import numpy as np
import ml_dtypes


def mxq(x, axis, fmt="e4m3"):
    dtype, down = {"e4m3": (ml_dtypes.float8_e4m3fn, 7), "e5m2": (ml_dtypes.float8_e5m2, 14)}[fmt]
    v = np.moveaxis(np.asarray(x, np.float32).astype(ml_dtypes.bfloat16).astype(np.float64), axis, -1)
    blocks = v.reshape(v.shape[:-1] + (-1, 32))
    amax = np.abs(blocks).max(-1, keepdims=True)
    byte = np.maximum(np.where(amax > 0, np.frexp(amax)[1] - 1 + 127, 0) - down, 1)
    scale = np.exp2(byte - 127.0)
    codes = (blocks / scale).astype(np.float32).astype(dtype).astype(np.float64)
    return np.moveaxis((codes * scale).reshape(v.shape), -1, axis)


WIDE = False


def mx_kscale(k):
    if not WIDE:
        return np.ones(k)
    levels = np.array([10, -10, 5, -5, 0])
    if k % 512:
        return np.exp2(np.random.permutation(np.resize(levels, k // 32))).repeat(32)
    a = np.empty((k // 512, 16))
    for p in range(k // 512):
        a[p, :8] = np.random.permutation(np.resize(levels, 8))
        for g in range(8):
            far = levels[np.abs(levels - a[p, g]) >= 10]
            a[p, g + 8] = far[np.random.randint(len(far))]
    return np.exp2(a.ravel()).repeat(32)


def f64(x):
    return np.asarray(x).astype(np.float64)


def striped(idx):
    return np.tile(idx.reshape(-1, 16).T, (8, 1)).astype(np.uint16)


def unstriped(offs):
    return offs[:16].T.reshape(-1).astype(np.int64)


def pack_weight(w):
    k, n = w.shape
    w = f64(np.asarray(w, np.float32).astype(ml_dtypes.bfloat16)).reshape(k // 32, 32, n)
    amax = np.abs(w).max(1)
    byte = np.clip(np.where(amax > 0, np.frexp(amax)[1] - 1 + 127 - 7, 1), 1, 254)
    scaled = (w * np.exp2(127.0 - byte)[:, None, :]).reshape(k, n).astype(np.float32)
    words = np.ascontiguousarray(scaled.reshape(k // 512, 128, 4, n).transpose(0, 1, 3, 2)).astype(ml_dtypes.float8_e4m3fn).view(np.uint8)
    return words, np.ascontiguousarray(byte.astype(np.uint8).reshape(k // 512, 16, n))


def unpack_weight(words, scales):
    g, p, n, _ = words.shape
    vals = np.ascontiguousarray(words).view(ml_dtypes.float8_e4m3fn).astype(np.float64) * np.repeat(np.exp2(scales.astype(np.float64) - 127.0), 8, axis=1)[..., None]
    return vals.transpose(0, 1, 3, 2).reshape(g * 512, n)


K, T, E, C, N = 1024, 512, 4, 128, 512


def by_expert(wq, xq):
    return np.concatenate([wq[e].T @ xq[:, e * C:(e + 1) * C] for e in range(E)], axis=1)


def setup_inputs():
    n = np.random.standard_normal
    s = mx_kscale(K)[:, None]
    packed = [pack_weight(m) for m in n((E, K, N)) / np.sqrt(K) / s[None]]
    return {
        "xT": (n((K, T)) * s).astype(np.float32),
        "w_words": np.stack([m[0] for m in packed]),
        "w_scales": np.stack([m[1] for m in packed]),
        "gate": np.tile(np.random.uniform(0.2, 1.0, E * C), (N, 1)).astype(np.float32),
        "offs": striped(np.random.permutation(T)[:E * C]),
    }


def reference(xT, w_words, w_scales, gate, offs):
    idx = unstriped(offs)
    xq = mxq(f64(xT)[:, idx], 0, "e4m3")
    w = np.stack([unpack_weight(w_words[e], w_scales[e]) for e in range(E)])
    y = by_expert(w, xq)
    out = np.zeros((N, T))
    out[:, idx] = f64(gate) * y
    return out

@@ -1,0 +1,148 @@
+from contextlib import ExitStack
+
+import concourse.mybir as mybir
+
+K, T, E, C, N = 1024, 512, 4, 128, 512
+FLOPS = 2 * K * N * E * C
+
+F32 = mybir.dt.float32
+BF16 = mybir.dt.bfloat16
+U32 = mybir.dt.uint32
+I32 = mybir.dt.int32
+U16 = mybir.dt.uint16
+U8 = mybir.dt.uint8
+FP8X4 = mybir.dt.float8_e4m3fn_x4
+MULT = mybir.AluOpType.mult
+
+P = 128
+PACK = 4
+PASSES = K // (P * PACK)
+NB = N // P
+H = 2
+S = E * C // H
+EH = E // H
+
+
+def tile_routed_moe_kernel(tc, xT, w_words, w_scales, gate, offs, out):
+    nc = tc.nc
+    with ExitStack() as ctx:
+        lists = ctx.enter_context(tc.tile_pool(name="lists", bufs=1))
+        keep = ctx.enter_context(tc.tile_pool(name="keep", bufs=1))
+        psum = ctx.enter_context(tc.psum_pool(name="psum", bufs=1))
+
+        offs_t = lists.tile([P, E * C // 16], U16, name="offs_t")
+        nc.sync.dma_start(offs_t[:], offs)
+
+        warm_in = keep.tile([P, 8], F32, name="warm_in")
+        warm_out = keep.tile([P, 8], F32, name="warm_out")
+        nc.vector.memset(warm_in[:], 0.0)
+        nc.scalar.copy(out=warm_out[:], in_=warm_in[:])
+
+        x_view = xT.rearrange("(g p t) n -> g p t n", p=P, t=PACK)
+        planes = {}
+        for g in range(PASSES):
+            for t in range(PACK):
+                planes[(g, t)] = keep.tile([P, T], F32, name="plane%d%d" % (g, t))
+                nc.sync.dma_start(planes[(g, t)][:], x_view[g, :, t, :])
+
+        w_sc = keep.tile([P, E * PASSES, N], U8, name="w_sc", align_bytes=64)
+        nc.vector.memset(w_sc[:].bitcast(I32), 0)
+        sc_view = w_scales.rearrange("e a (q r) n -> r q (e a) n", r=4)
+        for r in range(4):
+            nc.sync.dma_start(w_sc[r:P:32, :, :].bitcast(I32), sc_view[r].bitcast(I32))
+
+        w_cd = {}
+        gates = {}
+
+        def load_w(e):
+            w_cd[e] = keep.tile([P, PASSES, N], U32, name="w_cd%d" % e, align_bytes=64)
+            nc.sync.dma_start(w_cd[e][:].bitcast(I32), w_words[e].rearrange("a p n r -> p a (n r)").bitcast(I32))
+
+        def load_gate(b):
+            gates[b] = keep.tile([P, E * C], F32, name="gate%d" % b)
+            nc.sync.dma_start(gates[b][:], gate[b * P:(b + 1) * P, :])
+
+        load_w(0)
+        load_w(1)
+        load_gate(0)
+        load_w(2)
+        load_w(3)
+        for b in range(1, NB):
+            load_gate(b)
+
+        g4 = {}
+        xb = {}
+        x_cd = {}
+        x_sc = {}
+        acc = {}
+        y_sb = {}
+        win = [keep.tile([P, T], F32, name="win%d" % b) for b in range(NB)]
+
+        def sl(h):
+            return offs_t[:, h * (S // 16):(h + 1) * (S // 16)]
+
+        def gather(h, g):
+            g4[(h, g)] = keep.tile([P, PACK, S], F32, name="g4_%d%d" % (h, g))
+            for t in range(PACK):
+                nc.vector.tensor_copy(g4[(h, g)][:, t, :], planes[(g, t)][:].indirect(sl(h)))
+
+        def inter(h, g):
+            xb[(h, g)] = keep.tile([P, S, PACK], BF16, name="xb_%d%d" % (h, g), align_bytes=64)
+            nc.scalar.copy(out=xb[(h, g)][:], in_=g4[(h, g)][:].rearrange("p t n -> p n t"))
+
+        def quant(h, g):
+            x_cd[(h, g)] = keep.tile([P, S], U32, name="x_cd_%d%d" % (h, g), align_bytes=64)
+            x_sc[(h, g)] = keep.tile([P, S], U8, name="x_sc_%d%d" % (h, g), align_bytes=64)
+            nc.vector.quantize_mx(
+                out=x_cd[(h, g)][:].bitcast(FP8X4),
+                scales=x_sc[(h, g)][:],
+                in_=xb[(h, g)][:].rearrange("p n t -> p (n t)"),
+            )
+
+        def mm(h):
+            for b in range(NB):
+                acc[(h, b)] = psum.tile([P, 512], F32, name="acc_%d%d" % (h, b))
+                for el in range(EH):
+                    e = h * EH + el
+                    for g in range(PASSES):
+                        nc.tensor.matmul_mx(
+                            out=acc[(h, b)][:, el * C:(el + 1) * C],
+                            lhsT=w_cd[e][:, g, b * P:(b + 1) * P].bitcast(FP8X4),
+                            lhsT_scale=w_sc[:, e * PASSES + g, b * P:(b + 1) * P],
+                            rhs=x_cd[(h, g)][:, el * C:(el + 1) * C].bitcast(FP8X4),
+                            rhs_scale=x_sc[(h, g)][:, el * C:(el + 1) * C],
+                            start=(g == 0),
+                            stop=(g == PASSES - 1),
+                        )
+
+        def evac(h, b):
+            y_sb[(h, b)] = keep.tile([P, S], F32, name="y_%d%d" % (h, b))
+            nc.scalar.copy(out=y_sb[(h, b)][:], in_=acc[(h, b)][:, 0:S])
+
+        def scat(h, b):
+            nc.vector.tensor_tensor(win[b][:].indirect(sl(h)), y_sb[(h, b)][:], gates[b][:, h * S:(h + 1) * S], MULT)
+
+        gather(0, 0)
+        inter(0, 0)
+        gather(0, 1)
+        inter(0, 1)
+        quant(0, 0)
+        gather(1, 0)
+        inter(1, 0)
+        quant(0, 1)
+        mm(0)
+        for b in range(NB):
+            evac(0, b)
+        gather(1, 1)
+        inter(1, 1)
+        quant(1, 0)
+        scat(0, 0)
+        quant(1, 1)
+        mm(1)
+        for b in range(NB):
+            evac(1, b)
+        for b in range(1, NB):
+            scat(0, b)
+        for b in range(NB):
+            scat(1, b)
+            nc.sync.dma_start(out[b * P:(b + 1) * P, :], win[b][:])

@@ -13,14 +13,81 @@ U16 = mybir.dt.uint16
 U8 = mybir.dt.uint8
 FP8X4 = mybir.dt.float8_e4m3fn_x4
 MULT = mybir.AluOpType.mult
+ADD = mybir.AluOpType.add
+COPY = mybir.ActivationFunctionType.Copy
 
 P = 128
 PACK = 4
-PASSES = K // (P * PACK)
+PASSES = 2
 NB = N // P
-H = 2
-S = E * C // H
-EH = E // H
+J = E * C
+GWIN = 2048
+SWIN = 1024
+WIDE = ((0, 0), (0, 1), (0, 2))
+SLICES = ((0, 128), (128, 256), (256, 512))
+LOADS = ((0, 0), (1, 0), (0, 1), (1, 1), (0, 2), (1, 2), (0, 3), (1, 3))
+PROGRAM = (
+    ("cast", "s", 1, 0),
+    ("fgat", 1, 0, 256, 512),
+    ("gath", 0, 0, 0, 512),
+    ("cast", "s", 1, 1),
+    ("fgat", 1, 1, 256, 512),
+    ("gath", 0, 1, 0, 512),
+    ("cast", "s", 1, 2),
+    ("fgat", 1, 2, 256, 512),
+    ("gath", 0, 2, 0, 512),
+    ("gath", 0, 3, 0, 128),
+    ("inter", "s", 0, 0, 128),
+    ("gath", 1, 0, 0, 128),
+    ("gath", 1, 1, 0, 128),
+    ("gath", 1, 2, 0, 128),
+    ("gath", 1, 3, 0, 128),
+    ("inter", "s", 1, 0, 128),
+    ("gath", 0, 3, 128, 512),
+    ("cast", "s", 1, 3),
+    ("gath", 1, 0, 128, 256),
+    ("quant", 0),
+    ("mm", 0, 0, 128),
+    ("gath", 1, 1, 128, 256),
+    ("gath", 1, 2, 128, 256),
+    ("gath", 1, 3, 128, 256),
+    ("evac", 0, 128, 0),
+    ("evac", 0, 128, 1),
+    ("evac", 0, 128, 2),
+    ("evac", 0, 128, 3),
+    ("inter", "s", 0, 128, 256),
+    ("inter", "s", 1, 128, 256),
+    ("scat", 0, 128, 0),
+    ("scat", 0, 128, 1),
+    ("fgat", 1, 3, 256, 512),
+    ("quant", 128),
+    ("mm", 1, 128, 256),
+    ("scat", 0, 128, 2),
+    ("scat", 0, 128, 3),
+    ("evac", 128, 256, 0),
+    ("evac", 128, 256, 1),
+    ("evac", 128, 256, 2),
+    ("evac", 128, 256, 3),
+    ("inter", "s", 0, 256, 512),
+    ("scat", 128, 256, 0),
+    ("scat", 128, 256, 1),
+    ("quant", 256),
+    ("mm", 0, 256, 512),
+    ("scat", 128, 256, 2),
+    ("scat", 128, 256, 3),
+    ("evac", 256, 512, 0),
+    ("evac", 256, 512, 1),
+    ("evac", 256, 512, 2),
+    ("evac", 256, 512, 3),
+    ("scat", 256, 512, 0),
+    ("store", 0),
+    ("scat", 256, 512, 1),
+    ("store", 1),
+    ("scat", 256, 512, 2),
+    ("store", 2),
+    ("scat", 256, 512, 3),
+    ("store", 3),
+)
 
 
 def tile_routed_moe_kernel(tc, xT, w_words, w_scales, gate, offs, out):
@@ -30,20 +97,19 @@ def tile_routed_moe_kernel(tc, xT, w_words, w_scales, gate, offs, out):
         keep = ctx.enter_context(tc.tile_pool(name="keep", bufs=1))
         psum = ctx.enter_context(tc.psum_pool(name="psum", bufs=1))
 
-        offs_t = lists.tile([P, E * C // 16], U16, name="offs_t")
+        offs_t = lists.tile([P, J // 16], U16, name="offs_t")
         nc.sync.dma_start(offs_t[:], offs)
 
         warm_in = keep.tile([P, 8], F32, name="warm_in")
         warm_out = keep.tile([P, 8], F32, name="warm_out")
-        nc.vector.memset(warm_in[:], 0.0)
+        nc.gpsimd.memset(warm_in[:], 0.0)
         nc.scalar.copy(out=warm_out[:], in_=warm_in[:])
 
         x_view = xT.rearrange("(g p t) n -> g p t n", p=P, t=PACK)
         planes = {}
-        for g in range(PASSES):
-            for t in range(PACK):
-                planes[(g, t)] = keep.tile([P, T], F32, name="plane%d%d" % (g, t))
-                nc.sync.dma_start(planes[(g, t)][:], x_view[g, :, t, :])
+        for g, t in LOADS:
+            planes[(g, t)] = keep.tile([P, GWIN if (g, t) in WIDE else T], F32, name="plane%d%d" % (g, t))
+            nc.sync.dma_start(planes[(g, t)][:, 0:T], x_view[g, :, t, :])
 
         w_sc = keep.tile([P, E * PASSES, N], U8, name="w_sc", align_bytes=64)
         nc.vector.memset(w_sc[:].bitcast(I32), 0)
@@ -59,90 +125,86 @@ def tile_routed_moe_kernel(tc, xT, w_words, w_scales, gate, offs, out):
             nc.sync.dma_start(w_cd[e][:].bitcast(I32), w_words[e].rearrange("a p n r -> p a (n r)").bitcast(I32))
 
         def load_gate(b):
-            gates[b] = keep.tile([P, E * C], F32, name="gate%d" % b)
+            gates[b] = keep.tile([P, J], F32, name="gate%d" % b)
             nc.sync.dma_start(gates[b][:], gate[b * P:(b + 1) * P, :])
 
         load_w(0)
+        for b in range(NB):
+            load_gate(b)
         load_w(1)
-        load_gate(0)
         load_w(2)
         load_w(3)
-        for b in range(1, NB):
-            load_gate(b)
 
-        g4 = {}
+        g4 = [keep.tile([P, PACK, J], F32, name="g4_%d" % g) for g in range(PASSES)]
+        xbf = [keep.tile([P, PACK, T], BF16, name="xbf_%d" % g) for g in range(PASSES)]
         xb = {}
         x_cd = {}
         x_sc = {}
+        for j0, j1 in SLICES:
+            xb[j0] = keep.tile([P, PASSES, PACK * (j1 - j0)], BF16, name="xb_%d" % j0, align_bytes=64)
+            x_cd[j0] = keep.tile([P, PASSES, j1 - j0], U32, name="x_cd_%d" % j0, align_bytes=64)
+            x_sc[j0] = keep.tile([P, PASSES, j1 - j0], U8, name="x_sc_%d" % j0, align_bytes=64)
+        win = [keep.tile([P, SWIN], F32, name="win%d" % b) for b in range(NB)]
         acc = {}
         y_sb = {}
-        win = [keep.tile([P, T], F32, name="win%d" % b) for b in range(NB)]
 
-        def sl(h):
-            return offs_t[:, h * (S // 16):(h + 1) * (S // 16)]
+        def sl(j0, j1):
+            return offs_t[:, j0 // 16:j1 // 16]
 
-        def gather(h, g):
-            g4[(h, g)] = keep.tile([P, PACK, S], F32, name="g4_%d%d" % (h, g))
-            for t in range(PACK):
-                nc.vector.tensor_copy(g4[(h, g)][:, t, :], planes[(g, t)][:].indirect(sl(h)))
+        def gath(g, t, j0, j1):
+            nc.vector.tensor_copy(g4[g][:, t, j0:j1], planes[(g, t)][:].indirect(sl(j0, j1)))
 
-        def inter(h, g):
-            xb[(h, g)] = keep.tile([P, S, PACK], BF16, name="xb_%d%d" % (h, g), align_bytes=64)
-            nc.scalar.copy(out=xb[(h, g)][:], in_=g4[(h, g)][:].rearrange("p t n -> p n t"))
+        def cast(eng, g, t):
+            if eng == "s":
+                nc.scalar.copy(out=xbf[g][:, t, :], in_=planes[(g, t)][:, 0:T])
+            else:
+                nc.gpsimd.tensor_scalar(xbf[g][:, t, :], planes[(g, t)][:, 0:T], 1.0, 0.0, MULT, ADD)
 
-        def quant(h, g):
-            x_cd[(h, g)] = keep.tile([P, S], U32, name="x_cd_%d%d" % (h, g), align_bytes=64)
-            x_sc[(h, g)] = keep.tile([P, S], U8, name="x_sc_%d%d" % (h, g), align_bytes=64)
+        def fgat(g, t, j0, j1):
+            dst = xb[j0][:, g, :].rearrange("p (n t) -> p n t", t=PACK)
+            nc.scalar.activation(dst[:, :, t], xbf[g][:, t, :].indirect(sl(j0, j1)), COPY)
+
+        def inter(eng, g, j0, j1):
+            dst = xb[j0][:, g, :].rearrange("p (n t) -> p n t", t=PACK)
+            src = g4[g][:, :, j0:j1].rearrange("p t n -> p n t")
+            if eng == "s":
+                nc.scalar.copy(out=dst, in_=src)
+            else:
+                nc.gpsimd.tensor_scalar(dst, src, 1.0, 0.0, MULT, ADD)
+
+        def quant(j0):
             nc.vector.quantize_mx(
-                out=x_cd[(h, g)][:].bitcast(FP8X4),
-                scales=x_sc[(h, g)][:],
-                in_=xb[(h, g)][:].rearrange("p n t -> p (n t)"),
+                out=x_cd[j0][:].rearrange("p g n -> p (g n)").bitcast(FP8X4),
+                scales=x_sc[j0][:].rearrange("p g n -> p (g n)"),
+                in_=xb[j0][:].rearrange("p g c -> p (g c)"),
             )
 
-        def mm(h):
+        def mm(bank, j0, j1):
             for b in range(NB):
-                acc[(h, b)] = psum.tile([P, 512], F32, name="acc_%d%d" % (h, b))
-                for el in range(EH):
-                    e = h * EH + el
+                acc[(j0, b)] = psum.tile([P, 512], F32, name="acc_%d_%d" % (bank, b))
+                for e in range(j0 // C, j1 // C):
                     for g in range(PASSES):
                         nc.tensor.matmul_mx(
-                            out=acc[(h, b)][:, el * C:(el + 1) * C],
+                            out=acc[(j0, b)][:, e * C - j0:(e + 1) * C - j0],
                             lhsT=w_cd[e][:, g, b * P:(b + 1) * P].bitcast(FP8X4),
                             lhsT_scale=w_sc[:, e * PASSES + g, b * P:(b + 1) * P],
-                            rhs=x_cd[(h, g)][:, el * C:(el + 1) * C].bitcast(FP8X4),
-                            rhs_scale=x_sc[(h, g)][:, el * C:(el + 1) * C],
+                            rhs=x_cd[j0][:, g, e * C - j0:(e + 1) * C - j0].bitcast(FP8X4),
+                            rhs_scale=x_sc[j0][:, g, e * C - j0:(e + 1) * C - j0],
                             start=(g == 0),
                             stop=(g == PASSES - 1),
                         )
 
-        def evac(h, b):
-            y_sb[(h, b)] = keep.tile([P, S], F32, name="y_%d%d" % (h, b))
-            nc.scalar.copy(out=y_sb[(h, b)][:], in_=acc[(h, b)][:, 0:S])
+        def evac(j0, j1, b):
+            y_sb[(j0, b)] = keep.tile([P, j1 - j0], F32, name="y_%d_%d" % (j0, b))
+            nc.scalar.copy(out=y_sb[(j0, b)][:], in_=acc[(j0, b)][:, 0:j1 - j0])
 
-        def scat(h, b):
-            nc.vector.tensor_tensor(win[b][:].indirect(sl(h)), y_sb[(h, b)][:], gates[b][:, h * S:(h + 1) * S], MULT)
+        def scat(j0, j1, b):
+            nc.vector.tensor_tensor(win[b][:].indirect(sl(j0, j1)), y_sb[(j0, b)][:], gates[b][:, j0:j1], MULT)
 
-        gather(0, 0)
-        inter(0, 0)
-        gather(0, 1)
-        inter(0, 1)
-        quant(0, 0)
-        gather(1, 0)
-        inter(1, 0)
-        quant(0, 1)
-        mm(0)
-        for b in range(NB):
-            evac(0, b)
-        gather(1, 1)
-        inter(1, 1)
-        quant(1, 0)
-        scat(0, 0)
-        quant(1, 1)
-        mm(1)
-        for b in range(NB):
-            evac(1, b)
-        for b in range(1, NB):
-            scat(0, b)
-        for b in range(NB):
-            scat(1, b)
-            nc.sync.dma_start(out[b * P:(b + 1) * P, :], win[b][:])
+        def store(b):
+            nc.sync.dma_start(out[b * P:(b + 1) * P, :], win[b][:, 0:T])
+
+        ops = {"gath": gath, "cast": cast, "fgat": fgat, "inter": inter, "quant": quant,
+               "mm": mm, "evac": evac, "scat": scat, "store": store}
+        for step in PROGRAM:
+            ops[step[0]](*step[1:])

@@ -23,69 +23,83 @@ NB = N // P
 J = E * C
 GWIN = 2048
 SWIN = 1024
-WIDE = ((0, 0), (0, 1), (0, 2))
-SLICES = ((0, 128), (128, 256), (256, 512))
+WIDE = ((0, 0), (0, 1))
+SLICES = ((0, 128), (128, 256), (256, 384), (384, 512))
 LOADS = ((0, 0), (1, 0), (0, 1), (1, 1), (0, 2), (1, 2), (0, 3), (1, 3))
 PROGRAM = (
-    ("cast", "s", 1, 0),
-    ("fgat", 1, 0, 256, 512),
     ("gath", 0, 0, 0, 512),
-    ("cast", "s", 1, 1),
-    ("fgat", 1, 1, 256, 512),
+    ("cast", "s", 1, 0),
+    ("fgat", 1, 0, 0, 128),
     ("gath", 0, 1, 0, 512),
-    ("cast", "s", 1, 2),
-    ("fgat", 1, 2, 256, 512),
-    ("gath", 0, 2, 0, 512),
+    ("cast", "s", 1, 1),
+    ("fgat", 1, 1, 0, 128),
+    ("gath", 0, 2, 0, 128),
+    ("cast", "v", 1, 2),
+    ("fgat", 1, 2, 0, 128),
     ("gath", 0, 3, 0, 128),
     ("inter", "s", 0, 0, 128),
-    ("gath", 1, 0, 0, 128),
-    ("gath", 1, 1, 0, 128),
-    ("gath", 1, 2, 0, 128),
-    ("gath", 1, 3, 0, 128),
-    ("inter", "s", 1, 0, 128),
-    ("gath", 0, 3, 128, 512),
-    ("cast", "s", 1, 3),
-    ("gath", 1, 0, 128, 256),
+    ("cast", "v", 1, 3),
+    ("fgat", 1, 3, 0, 128),
+    ("gath", 0, 2, 128, 512),
     ("quant", 0),
     ("mm", 0, 0, 128),
-    ("gath", 1, 1, 128, 256),
-    ("gath", 1, 2, 128, 256),
-    ("gath", 1, 3, 128, 256),
+    ("gath", 0, 3, 128, 512),
     ("evac", 0, 128, 0),
-    ("evac", 0, 128, 1),
-    ("evac", 0, 128, 2),
-    ("evac", 0, 128, 3),
-    ("inter", "s", 0, 128, 256),
-    ("inter", "s", 1, 128, 256),
     ("scat", 0, 128, 0),
+    ("fgat", 1, 0, 128, 256),
+    ("fgat", 1, 1, 128, 256),
+    ("evac", 0, 128, 1),
+    ("fgat", 1, 2, 128, 256),
+    ("fgat", 1, 3, 128, 256),
+    ("evac", 0, 128, 2),
+    ("inter", "s", 0, 128, 256),
+    ("evac", 0, 128, 3),
     ("scat", 0, 128, 1),
-    ("fgat", 1, 3, 256, 512),
     ("quant", 128),
     ("mm", 1, 128, 256),
     ("scat", 0, 128, 2),
     ("scat", 0, 128, 3),
+    ("fgat", 1, 0, 256, 384),
+    ("fgat", 1, 1, 256, 384),
     ("evac", 128, 256, 0),
     ("evac", 128, 256, 1),
+    ("fgat", 1, 2, 256, 384),
+    ("fgat", 1, 3, 256, 384),
     ("evac", 128, 256, 2),
+    ("inter", "s", 0, 256, 384),
     ("evac", 128, 256, 3),
-    ("inter", "s", 0, 256, 512),
     ("scat", 128, 256, 0),
     ("scat", 128, 256, 1),
     ("quant", 256),
-    ("mm", 0, 256, 512),
+    ("mm", 0, 256, 384),
     ("scat", 128, 256, 2),
     ("scat", 128, 256, 3),
-    ("evac", 256, 512, 0),
-    ("evac", 256, 512, 1),
-    ("evac", 256, 512, 2),
-    ("evac", 256, 512, 3),
-    ("scat", 256, 512, 0),
+    ("fgat", 1, 0, 384, 512),
+    ("fgat", 1, 1, 384, 512),
+    ("evac", 256, 384, 0),
+    ("evac", 256, 384, 1),
+    ("fgat", 1, 2, 384, 512),
+    ("fgat", 1, 3, 384, 512),
+    ("evac", 256, 384, 2),
+    ("inter", "s", 0, 384, 512),
+    ("evac", 256, 384, 3),
+    ("scat", 256, 384, 0),
+    ("scat", 256, 384, 1),
+    ("quant", 384),
+    ("mm", 1, 384, 512),
+    ("scat", 256, 384, 2),
+    ("scat", 256, 384, 3),
+    ("evac", 384, 512, 0),
+    ("evac", 384, 512, 1),
+    ("evac", 384, 512, 2),
+    ("evac", 384, 512, 3),
+    ("scat", 384, 512, 0),
     ("store", 0),
-    ("scat", 256, 512, 1),
+    ("scat", 384, 512, 1),
     ("store", 1),
-    ("scat", 256, 512, 2),
+    ("scat", 384, 512, 2),
     ("store", 2),
-    ("scat", 256, 512, 3),
+    ("scat", 384, 512, 3),
     ("store", 3),
 )
 
@@ -95,6 +109,7 @@ def tile_routed_moe_kernel(tc, xT, w_words, w_scales, gate, offs, out):
     with ExitStack() as ctx:
         lists = ctx.enter_context(tc.tile_pool(name="lists", bufs=1))
         keep = ctx.enter_context(tc.tile_pool(name="keep", bufs=1))
+        ring = ctx.enter_context(tc.tile_pool(name="ring", bufs=2))
         psum = ctx.enter_context(tc.psum_pool(name="psum", bufs=1))
 
         offs_t = lists.tile([P, J // 16], U16, name="offs_t")
@@ -141,12 +156,16 @@ def tile_routed_moe_kernel(tc, xT, w_words, w_scales, gate, offs, out):
         x_cd = {}
         x_sc = {}
         for j0, j1 in SLICES:
-            xb[j0] = keep.tile([P, PASSES, PACK * (j1 - j0)], BF16, name="xb_%d" % j0, align_bytes=64)
             x_cd[j0] = keep.tile([P, PASSES, j1 - j0], U32, name="x_cd_%d" % j0, align_bytes=64)
             x_sc[j0] = keep.tile([P, PASSES, j1 - j0], U8, name="x_sc_%d" % j0, align_bytes=64)
         win = [keep.tile([P, SWIN], F32, name="win%d" % b) for b in range(NB)]
         acc = {}
         y_sb = {}
+
+        def xb_of(j0, j1):
+            if j0 not in xb:
+                xb[j0] = ring.tile([P, PASSES, PACK * (j1 - j0)], BF16, name="xb", align_bytes=64)
+            return xb[j0]
 
         def sl(j0, j1):
             return offs_t[:, j0 // 16:j1 // 16]
@@ -157,15 +176,17 @@ def tile_routed_moe_kernel(tc, xT, w_words, w_scales, gate, offs, out):
         def cast(eng, g, t):
             if eng == "s":
                 nc.scalar.copy(out=xbf[g][:, t, :], in_=planes[(g, t)][:, 0:T])
+            elif eng == "v":
+                nc.vector.tensor_copy(xbf[g][:, t, :], planes[(g, t)][:, 0:T])
             else:
                 nc.gpsimd.tensor_scalar(xbf[g][:, t, :], planes[(g, t)][:, 0:T], 1.0, 0.0, MULT, ADD)
 
         def fgat(g, t, j0, j1):
-            dst = xb[j0][:, g, :].rearrange("p (n t) -> p n t", t=PACK)
+            dst = xb_of(j0, j1)[:, g, :].rearrange("p (n t) -> p n t", t=PACK)
             nc.scalar.activation(dst[:, :, t], xbf[g][:, t, :].indirect(sl(j0, j1)), COPY)
 
         def inter(eng, g, j0, j1):
-            dst = xb[j0][:, g, :].rearrange("p (n t) -> p n t", t=PACK)
+            dst = xb_of(j0, j1)[:, g, :].rearrange("p (n t) -> p n t", t=PACK)
             src = g4[g][:, :, j0:j1].rearrange("p t n -> p n t")
             if eng == "s":
                 nc.scalar.copy(out=dst, in_=src)

@@ -23,83 +23,71 @@ NB = N // P
 J = E * C
 GWIN = 2048
 SWIN = 1024
-WIDE = ((0, 0), (0, 1))
-SLICES = ((0, 128), (128, 256), (256, 384), (384, 512))
+WIDE = ((0, 0), (0, 1), (0, 2))
 LOADS = ((0, 0), (1, 0), (0, 1), (1, 1), (0, 2), (1, 2), (0, 3), (1, 3))
 PROGRAM = (
-    ("gath", 0, 0, 0, 512),
     ("cast", "s", 1, 0),
-    ("fgat", 1, 0, 0, 128),
-    ("gath", 0, 1, 0, 512),
+    ("fgat", 1, 0, 256, 512),
+    ("gath", 0, 0, 0, 512),
     ("cast", "s", 1, 1),
-    ("fgat", 1, 1, 0, 128),
-    ("gath", 0, 2, 0, 128),
-    ("cast", "v", 1, 2),
-    ("fgat", 1, 2, 0, 128),
+    ("fgat", 1, 1, 256, 512),
+    ("gath", 0, 1, 0, 512),
+    ("cast", "s", 1, 2),
+    ("fgat", 1, 2, 256, 512),
+    ("gath", 0, 2, 0, 512),
     ("gath", 0, 3, 0, 128),
     ("inter", "s", 0, 0, 128),
-    ("cast", "v", 1, 3),
-    ("fgat", 1, 3, 0, 128),
-    ("gath", 0, 2, 128, 512),
-    ("quant", 0),
-    ("mm", 0, 0, 128),
+    ("gath", 1, 0, 0, 128),
+    ("gath", 1, 1, 0, 128),
+    ("gath", 1, 2, 0, 128),
+    ("gath", 1, 3, 0, 128),
+    ("inter", "s", 1, 0, 128),
     ("gath", 0, 3, 128, 512),
+    ("quant", 0, 0, 128),
+    ("cast", "s", 1, 3),
+    ("gath", 1, 0, 128, 256),
+    ("quant", 1, 0, 128),
+    ("mm", 0, 0, 128),
+    ("gath", 1, 1, 128, 256),
+    ("gath", 1, 2, 128, 256),
+    ("gath", 1, 3, 128, 256),
     ("evac", 0, 128, 0),
-    ("scat", 0, 128, 0),
-    ("fgat", 1, 0, 128, 256),
-    ("fgat", 1, 1, 128, 256),
     ("evac", 0, 128, 1),
-    ("fgat", 1, 2, 128, 256),
-    ("fgat", 1, 3, 128, 256),
     ("evac", 0, 128, 2),
-    ("inter", "s", 0, 128, 256),
     ("evac", 0, 128, 3),
+    ("inter", "s", 0, 128, 256),
+    ("inter", "s", 1, 128, 256),
+    ("scat", 0, 128, 0),
     ("scat", 0, 128, 1),
-    ("quant", 128),
+    ("fgat", 1, 3, 256, 512),
+    ("quant", 0, 128, 256),
+    ("quant", 1, 128, 256),
     ("mm", 1, 128, 256),
     ("scat", 0, 128, 2),
     ("scat", 0, 128, 3),
-    ("fgat", 1, 0, 256, 384),
-    ("fgat", 1, 1, 256, 384),
     ("evac", 128, 256, 0),
     ("evac", 128, 256, 1),
-    ("fgat", 1, 2, 256, 384),
-    ("fgat", 1, 3, 256, 384),
     ("evac", 128, 256, 2),
-    ("inter", "s", 0, 256, 384),
     ("evac", 128, 256, 3),
+    ("inter", "s", 0, 256, 512),
     ("scat", 128, 256, 0),
     ("scat", 128, 256, 1),
-    ("quant", 256),
-    ("mm", 0, 256, 384),
+    ("quant", 0, 256, 512),
+    ("quant", 1, 256, 512),
+    ("mm", 0, 256, 512),
     ("scat", 128, 256, 2),
     ("scat", 128, 256, 3),
-    ("fgat", 1, 0, 384, 512),
-    ("fgat", 1, 1, 384, 512),
-    ("evac", 256, 384, 0),
-    ("evac", 256, 384, 1),
-    ("fgat", 1, 2, 384, 512),
-    ("fgat", 1, 3, 384, 512),
-    ("evac", 256, 384, 2),
-    ("inter", "s", 0, 384, 512),
-    ("evac", 256, 384, 3),
-    ("scat", 256, 384, 0),
-    ("scat", 256, 384, 1),
-    ("quant", 384),
-    ("mm", 1, 384, 512),
-    ("scat", 256, 384, 2),
-    ("scat", 256, 384, 3),
-    ("evac", 384, 512, 0),
-    ("evac", 384, 512, 1),
-    ("evac", 384, 512, 2),
-    ("evac", 384, 512, 3),
-    ("scat", 384, 512, 0),
+    ("evac", 256, 512, 0),
+    ("evac", 256, 512, 1),
+    ("evac", 256, 512, 2),
+    ("evac", 256, 512, 3),
+    ("scat", 256, 512, 0),
     ("store", 0),
-    ("scat", 384, 512, 1),
+    ("scat", 256, 512, 1),
     ("store", 1),
-    ("scat", 384, 512, 2),
+    ("scat", 256, 512, 2),
     ("store", 2),
-    ("scat", 384, 512, 3),
+    ("scat", 256, 512, 3),
     ("store", 3),
 )
 
@@ -109,7 +97,6 @@ def tile_routed_moe_kernel(tc, xT, w_words, w_scales, gate, offs, out):
     with ExitStack() as ctx:
         lists = ctx.enter_context(tc.tile_pool(name="lists", bufs=1))
         keep = ctx.enter_context(tc.tile_pool(name="keep", bufs=1))
-        ring = ctx.enter_context(tc.tile_pool(name="ring", bufs=2))
         psum = ctx.enter_context(tc.psum_pool(name="psum", bufs=1))
 
         offs_t = lists.tile([P, J // 16], U16, name="offs_t")
@@ -152,20 +139,12 @@ def tile_routed_moe_kernel(tc, xT, w_words, w_scales, gate, offs, out):
 
         g4 = [keep.tile([P, PACK, J], F32, name="g4_%d" % g) for g in range(PASSES)]
         xbf = [keep.tile([P, PACK, T], BF16, name="xbf_%d" % g) for g in range(PASSES)]
-        xb = {}
-        x_cd = {}
-        x_sc = {}
-        for j0, j1 in SLICES:
-            x_cd[j0] = keep.tile([P, PASSES, j1 - j0], U32, name="x_cd_%d" % j0, align_bytes=64)
-            x_sc[j0] = keep.tile([P, PASSES, j1 - j0], U8, name="x_sc_%d" % j0, align_bytes=64)
+        xb = [keep.tile([P, PACK * J], BF16, name="xb_%d" % g, align_bytes=64) for g in range(PASSES)]
+        x_cd = [keep.tile([P, J], U32, name="x_cd_%d" % g, align_bytes=64) for g in range(PASSES)]
+        x_sc = [keep.tile([P, J], U8, name="x_sc_%d" % g, align_bytes=64) for g in range(PASSES)]
         win = [keep.tile([P, SWIN], F32, name="win%d" % b) for b in range(NB)]
         acc = {}
         y_sb = {}
-
-        def xb_of(j0, j1):
-            if j0 not in xb:
-                xb[j0] = ring.tile([P, PASSES, PACK * (j1 - j0)], BF16, name="xb", align_bytes=64)
-            return xb[j0]
 
         def sl(j0, j1):
             return offs_t[:, j0 // 16:j1 // 16]
@@ -176,28 +155,26 @@ def tile_routed_moe_kernel(tc, xT, w_words, w_scales, gate, offs, out):
         def cast(eng, g, t):
             if eng == "s":
                 nc.scalar.copy(out=xbf[g][:, t, :], in_=planes[(g, t)][:, 0:T])
-            elif eng == "v":
-                nc.vector.tensor_copy(xbf[g][:, t, :], planes[(g, t)][:, 0:T])
             else:
                 nc.gpsimd.tensor_scalar(xbf[g][:, t, :], planes[(g, t)][:, 0:T], 1.0, 0.0, MULT, ADD)
 
         def fgat(g, t, j0, j1):
-            dst = xb_of(j0, j1)[:, g, :].rearrange("p (n t) -> p n t", t=PACK)
+            dst = xb[g][:, PACK * j0:PACK * j1].rearrange("p (n t) -> p n t", t=PACK)
             nc.scalar.activation(dst[:, :, t], xbf[g][:, t, :].indirect(sl(j0, j1)), COPY)
 
         def inter(eng, g, j0, j1):
-            dst = xb_of(j0, j1)[:, g, :].rearrange("p (n t) -> p n t", t=PACK)
+            dst = xb[g][:, PACK * j0:PACK * j1].rearrange("p (n t) -> p n t", t=PACK)
             src = g4[g][:, :, j0:j1].rearrange("p t n -> p n t")
             if eng == "s":
                 nc.scalar.copy(out=dst, in_=src)
             else:
                 nc.gpsimd.tensor_scalar(dst, src, 1.0, 0.0, MULT, ADD)
 
-        def quant(j0):
+        def quant(g, j0, j1):
             nc.vector.quantize_mx(
-                out=x_cd[j0][:].rearrange("p g n -> p (g n)").bitcast(FP8X4),
-                scales=x_sc[j0][:].rearrange("p g n -> p (g n)"),
-                in_=xb[j0][:].rearrange("p g c -> p (g c)"),
+                out=x_cd[g][:, j0:j1].bitcast(FP8X4),
+                scales=x_sc[g][:, j0:j1],
+                in_=xb[g][:, PACK * j0:PACK * j1],
             )
 
         def mm(bank, j0, j1):
@@ -209,8 +186,8 @@ def tile_routed_moe_kernel(tc, xT, w_words, w_scales, gate, offs, out):
                             out=acc[(j0, b)][:, e * C - j0:(e + 1) * C - j0],
                             lhsT=w_cd[e][:, g, b * P:(b + 1) * P].bitcast(FP8X4),
                             lhsT_scale=w_sc[:, e * PASSES + g, b * P:(b + 1) * P],
-                            rhs=x_cd[j0][:, g, e * C - j0:(e + 1) * C - j0].bitcast(FP8X4),
-                            rhs_scale=x_sc[j0][:, g, e * C - j0:(e + 1) * C - j0],
+                            rhs=x_cd[g][:, e * C:(e + 1) * C].bitcast(FP8X4),
+                            rhs_scale=x_sc[g][:, e * C:(e + 1) * C],
                             start=(g == 0),
                             stop=(g == PASSES - 1),
                         )

@@ -13,83 +13,26 @@ U16 = mybir.dt.uint16
 U8 = mybir.dt.uint8
 FP8X4 = mybir.dt.float8_e4m3fn_x4
 MULT = mybir.AluOpType.mult
-ADD = mybir.AluOpType.add
 COPY = mybir.ActivationFunctionType.Copy
 
 P = 128
 PACK = 4
-PASSES = 2
-NB = N // P
-J = E * C
-GWIN = 2048
-SWIN = 1024
-WIDE = ((0, 0), (0, 1), (0, 2))
-LOADS = ((0, 0), (1, 0), (0, 1), (1, 1), (0, 2), (1, 2), (0, 3), (1, 3))
-PROGRAM = (
-    ("cast", "s", 1, 0),
-    ("fgat", 1, 0, 256, 512),
-    ("gath", 0, 0, 0, 512),
-    ("cast", "s", 1, 1),
-    ("fgat", 1, 1, 256, 512),
-    ("gath", 0, 1, 0, 512),
-    ("cast", "s", 1, 2),
-    ("fgat", 1, 2, 256, 512),
-    ("gath", 0, 2, 0, 512),
-    ("gath", 0, 3, 0, 128),
-    ("inter", "s", 0, 0, 128),
-    ("gath", 1, 0, 0, 128),
-    ("gath", 1, 1, 0, 128),
-    ("gath", 1, 2, 0, 128),
-    ("gath", 1, 3, 0, 128),
-    ("inter", "s", 1, 0, 128),
-    ("gath", 0, 3, 128, 512),
-    ("quant", 0, 0, 128),
-    ("cast", "s", 1, 3),
-    ("gath", 1, 0, 128, 256),
-    ("quant", 1, 0, 128),
-    ("mm", 0, 0, 128),
-    ("gath", 1, 1, 128, 256),
-    ("gath", 1, 2, 128, 256),
-    ("gath", 1, 3, 128, 256),
-    ("evac", 0, 128, 0),
-    ("evac", 0, 128, 1),
-    ("evac", 0, 128, 2),
-    ("evac", 0, 128, 3),
-    ("inter", "s", 0, 128, 256),
-    ("inter", "s", 1, 128, 256),
-    ("scat", 0, 128, 0),
-    ("scat", 0, 128, 1),
-    ("fgat", 1, 3, 256, 512),
-    ("quant", 0, 128, 256),
-    ("quant", 1, 128, 256),
-    ("mm", 1, 128, 256),
-    ("scat", 0, 128, 2),
-    ("scat", 0, 128, 3),
-    ("evac", 128, 256, 0),
-    ("evac", 128, 256, 1),
-    ("evac", 128, 256, 2),
-    ("evac", 128, 256, 3),
-    ("inter", "s", 0, 256, 512),
-    ("scat", 128, 256, 0),
-    ("scat", 128, 256, 1),
-    ("quant", 0, 256, 512),
-    ("quant", 1, 256, 512),
-    ("mm", 0, 256, 512),
-    ("scat", 128, 256, 2),
-    ("scat", 128, 256, 3),
-    ("evac", 256, 512, 0),
-    ("evac", 256, 512, 1),
-    ("evac", 256, 512, 2),
-    ("evac", 256, 512, 3),
-    ("scat", 256, 512, 0),
-    ("store", 0),
-    ("scat", 256, 512, 1),
-    ("store", 1),
-    ("scat", 256, 512, 2),
-    ("store", 2),
-    ("scat", 256, 512, 3),
-    ("store", 3),
-)
+PASSES = K // (P * PACK)
+BLOCKS = N // P
+SLOTS = E * C
+PER_COLUMN = 16
+
+FIRST = (0, 128)
+SECOND = (128, 256)
+LAST = (256, 512)
+AFTER_FIRST = (128, 512)
+WHOLE = (0, 512)
+
+WIDE_GATHER_WINDOW = 4 * T
+SCATTER_WINDOW = 2 * T
+
+LOAD_ORDER = ((0, 0), (1, 0), (0, 1), (1, 1), (0, 2), (1, 2), (0, 3), (1, 3))
+WHOLE_LIST_PLANES = ((0, 0), (0, 1), (0, 2))
 
 
 def tile_routed_moe_kernel(tc, xT, w_words, w_scales, gate, offs, out):
@@ -99,110 +42,147 @@ def tile_routed_moe_kernel(tc, xT, w_words, w_scales, gate, offs, out):
         keep = ctx.enter_context(tc.tile_pool(name="keep", bufs=1))
         psum = ctx.enter_context(tc.psum_pool(name="psum", bufs=1))
 
-        offs_t = lists.tile([P, J // 16], U16, name="offs_t")
-        nc.sync.dma_start(offs_t[:], offs)
+        offsets = lists.tile([P, SLOTS // PER_COLUMN], U16, name="offsets")
+        nc.sync.dma_start(offsets[:], offs)
 
-        warm_in = keep.tile([P, 8], F32, name="warm_in")
-        warm_out = keep.tile([P, 8], F32, name="warm_out")
-        nc.gpsimd.memset(warm_in[:], 0.0)
-        nc.scalar.copy(out=warm_out[:], in_=warm_in[:])
+        scrap_in = keep.tile([P, 8], F32, name="scrap_in")
+        scrap_out = keep.tile([P, 8], F32, name="scrap_out")
+        nc.gpsimd.memset(scrap_in[:], 0.0)
+        nc.scalar.copy(out=scrap_out[:], in_=scrap_in[:])
 
-        x_view = xT.rearrange("(g p t) n -> g p t n", p=P, t=PACK)
-        planes = {}
-        for g, t in LOADS:
-            planes[(g, t)] = keep.tile([P, GWIN if (g, t) in WIDE else T], F32, name="plane%d%d" % (g, t))
-            nc.sync.dma_start(planes[(g, t)][:, 0:T], x_view[g, :, t, :])
+        x_planes = xT.rearrange("(g p t) n -> g p t n", p=P, t=PACK)
+        plane = {}
+        for g, t in LOAD_ORDER:
+            columns = WIDE_GATHER_WINDOW if (g, t) in WHOLE_LIST_PLANES else T
+            plane[(g, t)] = keep.tile([P, columns], F32, name="plane%d%d" % (g, t))
+            nc.sync.dma_start(plane[(g, t)][:, 0:T], x_planes[g, :, t, :])
 
-        w_sc = keep.tile([P, E * PASSES, N], U8, name="w_sc", align_bytes=64)
-        nc.vector.memset(w_sc[:].bitcast(I32), 0)
-        sc_view = w_scales.rearrange("e a (q r) n -> r q (e a) n", r=4)
+        w_scale = keep.tile([P, E * PASSES, N], U8, name="w_scale", align_bytes=64)
+        nc.vector.memset(w_scale[:].bitcast(I32), 0)
+        scale_rows = w_scales.rearrange("e a (q r) n -> r q (e a) n", r=4)
         for r in range(4):
-            nc.sync.dma_start(w_sc[r:P:32, :, :].bitcast(I32), sc_view[r].bitcast(I32))
+            nc.sync.dma_start(w_scale[r:P:32, :, :].bitcast(I32), scale_rows[r].bitcast(I32))
 
-        w_cd = {}
-        gates = {}
+        w_code = {}
+        gate_sb = {}
 
-        def load_w(e):
-            w_cd[e] = keep.tile([P, PASSES, N], U32, name="w_cd%d" % e, align_bytes=64)
-            nc.sync.dma_start(w_cd[e][:].bitcast(I32), w_words[e].rearrange("a p n r -> p a (n r)").bitcast(I32))
+        def load_codes(e):
+            w_code[e] = keep.tile([P, PASSES, N], U32, name="w_code%d" % e, align_bytes=64)
+            nc.sync.dma_start(w_code[e][:].bitcast(I32), w_words[e].rearrange("a p n r -> p a (n r)").bitcast(I32))
 
-        def load_gate(b):
-            gates[b] = keep.tile([P, J], F32, name="gate%d" % b)
-            nc.sync.dma_start(gates[b][:], gate[b * P:(b + 1) * P, :])
+        load_codes(0)
+        for b in range(BLOCKS):
+            gate_sb[b] = keep.tile([P, SLOTS], F32, name="gate%d" % b)
+            nc.sync.dma_start(gate_sb[b][:], gate[b * P:(b + 1) * P, :])
+        for e in range(1, E):
+            load_codes(e)
 
-        load_w(0)
-        for b in range(NB):
-            load_gate(b)
-        load_w(1)
-        load_w(2)
-        load_w(3)
+        gathered = [
+            keep.tile([P, PACK, SLOTS], F32, name="gathered0"),
+            keep.tile([P, PACK, LAST[0]], F32, name="gathered1"),
+        ]
+        plane_bf16 = keep.tile([P, PACK, T], BF16, name="plane_bf16")
+        interleaved = [keep.tile([P, PACK * SLOTS], BF16, name="interleaved%d" % g, align_bytes=64) for g in range(PASSES)]
+        x_code = [keep.tile([P, SLOTS], U32, name="x_code%d" % g, align_bytes=64) for g in range(PASSES)]
+        x_scale = [keep.tile([P, SLOTS], U8, name="x_scale%d" % g, align_bytes=64) for g in range(PASSES)]
+        window = [keep.tile([P, SCATTER_WINDOW], F32, name="window%d" % b) for b in range(BLOCKS)]
+        sums = {}
+        sums_sb = {}
 
-        g4 = [keep.tile([P, PACK, J], F32, name="g4_%d" % g) for g in range(PASSES)]
-        xbf = [keep.tile([P, PACK, T], BF16, name="xbf_%d" % g) for g in range(PASSES)]
-        xb = [keep.tile([P, PACK * J], BF16, name="xb_%d" % g, align_bytes=64) for g in range(PASSES)]
-        x_cd = [keep.tile([P, J], U32, name="x_cd_%d" % g, align_bytes=64) for g in range(PASSES)]
-        x_sc = [keep.tile([P, J], U8, name="x_sc_%d" % g, align_bytes=64) for g in range(PASSES)]
-        win = [keep.tile([P, SWIN], F32, name="win%d" % b) for b in range(NB)]
-        acc = {}
-        y_sb = {}
+        def offsets_of(piece):
+            return offsets[:, piece[0] // PER_COLUMN:piece[1] // PER_COLUMN]
 
-        def sl(j0, j1):
-            return offs_t[:, j0 // 16:j1 // 16]
+        def by_slot(g, piece):
+            return interleaved[g][:, PACK * piece[0]:PACK * piece[1]].rearrange("p (j t) -> p j t", t=PACK)
 
-        def gath(g, t, j0, j1):
-            nc.vector.tensor_copy(g4[g][:, t, j0:j1], planes[(g, t)][:].indirect(sl(j0, j1)))
+        def gather_f32(g, t, piece):
+            nc.vector.tensor_copy(gathered[g][:, t, piece[0]:piece[1]], plane[(g, t)][:].indirect(offsets_of(piece)))
 
-        def cast(eng, g, t):
-            if eng == "s":
-                nc.scalar.copy(out=xbf[g][:, t, :], in_=planes[(g, t)][:, 0:T])
-            else:
-                nc.gpsimd.tensor_scalar(xbf[g][:, t, :], planes[(g, t)][:, 0:T], 1.0, 0.0, MULT, ADD)
+        def round_plane(t):
+            nc.scalar.copy(out=plane_bf16[:, t, :], in_=plane[(1, t)][:])
 
-        def fgat(g, t, j0, j1):
-            dst = xb[g][:, PACK * j0:PACK * j1].rearrange("p (n t) -> p n t", t=PACK)
-            nc.scalar.activation(dst[:, :, t], xbf[g][:, t, :].indirect(sl(j0, j1)), COPY)
+        def gather_bf16(t, piece):
+            nc.scalar.activation(by_slot(1, piece)[:, :, t], plane_bf16[:, t, :].indirect(offsets_of(piece)), COPY)
 
-        def inter(eng, g, j0, j1):
-            dst = xb[g][:, PACK * j0:PACK * j1].rearrange("p (n t) -> p n t", t=PACK)
-            src = g4[g][:, :, j0:j1].rearrange("p t n -> p n t")
-            if eng == "s":
-                nc.scalar.copy(out=dst, in_=src)
-            else:
-                nc.gpsimd.tensor_scalar(dst, src, 1.0, 0.0, MULT, ADD)
+        def interleave(g, piece):
+            nc.scalar.copy(out=by_slot(g, piece), in_=gathered[g][:, :, piece[0]:piece[1]].rearrange("p t j -> p j t"))
 
-        def quant(g, j0, j1):
+        def quantize(g, piece):
             nc.vector.quantize_mx(
-                out=x_cd[g][:, j0:j1].bitcast(FP8X4),
-                scales=x_sc[g][:, j0:j1],
-                in_=xb[g][:, PACK * j0:PACK * j1],
+                out=x_code[g][:, piece[0]:piece[1]].bitcast(FP8X4),
+                scales=x_scale[g][:, piece[0]:piece[1]],
+                in_=interleaved[g][:, PACK * piece[0]:PACK * piece[1]],
             )
 
-        def mm(bank, j0, j1):
-            for b in range(NB):
-                acc[(j0, b)] = psum.tile([P, 512], F32, name="acc_%d_%d" % (bank, b))
-                for e in range(j0 // C, j1 // C):
+        def multiply(piece, banks):
+            for b in range(BLOCKS):
+                sums[(piece, b)] = psum.tile([P, 512], F32, name="sums_%d_%d" % (banks, b))
+                for e in range(piece[0] // C, piece[1] // C):
+                    slots = slice(e * C, (e + 1) * C)
                     for g in range(PASSES):
                         nc.tensor.matmul_mx(
-                            out=acc[(j0, b)][:, e * C - j0:(e + 1) * C - j0],
-                            lhsT=w_cd[e][:, g, b * P:(b + 1) * P].bitcast(FP8X4),
-                            lhsT_scale=w_sc[:, e * PASSES + g, b * P:(b + 1) * P],
-                            rhs=x_cd[g][:, e * C:(e + 1) * C].bitcast(FP8X4),
-                            rhs_scale=x_sc[g][:, e * C:(e + 1) * C],
+                            out=sums[(piece, b)][:, e * C - piece[0]:(e + 1) * C - piece[0]],
+                            lhsT=w_code[e][:, g, b * P:(b + 1) * P].bitcast(FP8X4),
+                            lhsT_scale=w_scale[:, e * PASSES + g, b * P:(b + 1) * P],
+                            rhs=x_code[g][:, slots].bitcast(FP8X4),
+                            rhs_scale=x_scale[g][:, slots],
                             start=(g == 0),
                             stop=(g == PASSES - 1),
                         )
 
-        def evac(j0, j1, b):
-            y_sb[(j0, b)] = keep.tile([P, j1 - j0], F32, name="y_%d_%d" % (j0, b))
-            nc.scalar.copy(out=y_sb[(j0, b)][:], in_=acc[(j0, b)][:, 0:j1 - j0])
+        def copy_out(piece):
+            for b in range(BLOCKS):
+                sums_sb[(piece, b)] = keep.tile([P, piece[1] - piece[0]], F32, name="sums_sb_%d_%d" % (piece[0], b))
+                nc.scalar.copy(out=sums_sb[(piece, b)][:], in_=sums[(piece, b)][:, 0:piece[1] - piece[0]])
 
-        def scat(j0, j1, b):
-            nc.vector.tensor_tensor(win[b][:].indirect(sl(j0, j1)), y_sb[(j0, b)][:], gates[b][:, j0:j1], MULT)
+        def scatter(piece, b):
+            nc.vector.tensor_tensor(
+                window[b][:].indirect(offsets_of(piece)), sums_sb[(piece, b)][:], gate_sb[b][:, piece[0]:piece[1]], MULT
+            )
 
-        def store(b):
-            nc.sync.dma_start(out[b * P:(b + 1) * P, :], win[b][:, 0:T])
 
-        ops = {"gath": gath, "cast": cast, "fgat": fgat, "inter": inter, "quant": quant,
-               "mm": mm, "evac": evac, "scat": scat, "store": store}
-        for step in PROGRAM:
-            ops[step[0]](*step[1:])
+        for t in range(PACK - 1):
+            round_plane(t)
+            gather_bf16(t, LAST)
+            gather_f32(0, t, WHOLE)
+
+        gather_f32(0, PACK - 1, FIRST)
+        interleave(0, FIRST)
+        for t in range(PACK):
+            gather_f32(1, t, FIRST)
+        interleave(1, FIRST)
+        gather_f32(0, PACK - 1, AFTER_FIRST)
+        quantize(0, FIRST)
+        round_plane(PACK - 1)
+        gather_f32(1, 0, SECOND)
+        quantize(1, FIRST)
+        multiply(FIRST, 0)
+        for t in range(1, PACK):
+            gather_f32(1, t, SECOND)
+        copy_out(FIRST)
+
+        interleave(0, SECOND)
+        interleave(1, SECOND)
+        scatter(FIRST, 0)
+        scatter(FIRST, 1)
+        gather_bf16(PACK - 1, LAST)
+        quantize(0, SECOND)
+        quantize(1, SECOND)
+        multiply(SECOND, 1)
+        scatter(FIRST, 2)
+        scatter(FIRST, 3)
+        copy_out(SECOND)
+
+        interleave(0, LAST)
+        scatter(SECOND, 0)
+        scatter(SECOND, 1)
+        quantize(0, LAST)
+        quantize(1, LAST)
+        multiply(LAST, 0)
+        scatter(SECOND, 2)
+        scatter(SECOND, 3)
+        copy_out(LAST)
+
+        for b in range(BLOCKS):
+            scatter(LAST, b)
+            nc.sync.dma_start(out[b * P:(b + 1) * P, :], window[b][:, 0:T])

@@ -31,7 +31,7 @@ WHOLE = (0, 512)
 WIDE_GATHER_WINDOW = 4 * T
 SCATTER_WINDOW = 2 * T
 
-LOAD_ORDER = ((0, 0), (1, 0), (0, 1), (1, 1), (0, 2), (1, 2), (0, 3), (1, 3))
+LOAD_ORDER = ((0, 0), (1, 0), (1, 1), (0, 1), (1, 2), (1, 3), (0, 2), (0, 3))
 WHOLE_LIST_PLANES = ((0, 0), (0, 1), (0, 2))
 
 
@@ -70,16 +70,21 @@ def tile_routed_moe_kernel(tc, xT, w_words, w_scales, gate, offs, out):
             w_code[e] = keep.tile([P, PASSES, N], U32, name="w_code%d" % e, align_bytes=64)
             nc.sync.dma_start(w_code[e][:].bitcast(I32), w_words[e].rearrange("a p n r -> p a (n r)").bitcast(I32))
 
+        gate_blocks = gate.rearrange("(b p) j -> p b j", p=P)
+
+        def load_gate(first, end):
+            gate_sb[first] = keep.tile([P, BLOCKS, end - first], F32, name="gate%d" % first)
+            nc.sync.dma_start(gate_sb[first][:], gate_blocks[:, :, first:end])
+
         load_codes(0)
-        for b in range(BLOCKS):
-            gate_sb[b] = keep.tile([P, SLOTS], F32, name="gate%d" % b)
-            nc.sync.dma_start(gate_sb[b][:], gate[b * P:(b + 1) * P, :])
+        load_gate(0, LAST[0])
         for e in range(1, E):
             load_codes(e)
+        load_gate(LAST[0], SLOTS)
 
         gathered = [
             keep.tile([P, PACK, SLOTS], F32, name="gathered0"),
-            keep.tile([P, PACK, LAST[0]], F32, name="gathered1"),
+            keep.tile([P, PACK, SLOTS], F32, name="gathered1"),
         ]
         plane_bf16 = keep.tile([P, PACK, T], BF16, name="plane_bf16")
         interleaved = [keep.tile([P, PACK * SLOTS], BF16, name="interleaved%d" % g, align_bytes=64) for g in range(PASSES)]
@@ -135,52 +140,48 @@ def tile_routed_moe_kernel(tc, xT, w_words, w_scales, gate, offs, out):
                 sums_sb[(piece, b)] = keep.tile([P, piece[1] - piece[0]], F32, name="sums_sb_%d_%d" % (piece[0], b))
                 nc.scalar.copy(out=sums_sb[(piece, b)][:], in_=sums[(piece, b)][:, 0:piece[1] - piece[0]])
 
+        def gate_of(piece, b):
+            first = 0 if piece[0] < LAST[0] else LAST[0]
+            return gate_sb[first][:, b, piece[0] - first:piece[1] - first]
+
         def scatter(piece, b):
             nc.vector.tensor_tensor(
-                window[b][:].indirect(offsets_of(piece)), sums_sb[(piece, b)][:], gate_sb[b][:, piece[0]:piece[1]], MULT
+                window[b][:].indirect(offsets_of(piece)), sums_sb[(piece, b)][:], gate_of(piece, b), MULT
             )
 
 
-        for t in range(PACK - 1):
-            round_plane(t)
-            gather_bf16(t, LAST)
-            gather_f32(0, t, WHOLE)
-
-        gather_f32(0, PACK - 1, FIRST)
-        interleave(0, FIRST)
+        gather_f32(0, 0, WHOLE)
         for t in range(PACK):
-            gather_f32(1, t, FIRST)
-        interleave(1, FIRST)
-        gather_f32(0, PACK - 1, AFTER_FIRST)
+            round_plane(t)
+            gather_bf16(t, FIRST)
+            gather_bf16(t, SECOND)
+        gather_f32(0, 1, WHOLE)
+        gather_f32(0, 2, WHOLE)
+        gather_f32(0, 3, FIRST)
+        interleave(0, FIRST)
         quantize(0, FIRST)
-        round_plane(PACK - 1)
-        gather_f32(1, 0, SECOND)
         quantize(1, FIRST)
         multiply(FIRST, 0)
-        for t in range(1, PACK):
-            gather_f32(1, t, SECOND)
         copy_out(FIRST)
 
+        gather_f32(0, 3, AFTER_FIRST)
+        for t in range(PACK):
+            gather_f32(1, t, LAST)
         interleave(0, SECOND)
-        interleave(1, SECOND)
-        scatter(FIRST, 0)
-        scatter(FIRST, 1)
-        gather_bf16(PACK - 1, LAST)
         quantize(0, SECOND)
         quantize(1, SECOND)
         multiply(SECOND, 1)
-        scatter(FIRST, 2)
-        scatter(FIRST, 3)
+        for b in range(BLOCKS):
+            scatter(FIRST, b)
         copy_out(SECOND)
 
         interleave(0, LAST)
-        scatter(SECOND, 0)
-        scatter(SECOND, 1)
+        interleave(1, LAST)
         quantize(0, LAST)
         quantize(1, LAST)
         multiply(LAST, 0)
-        scatter(SECOND, 2)
-        scatter(SECOND, 3)
+        for b in range(BLOCKS):
+            scatter(SECOND, b)
         copy_out(LAST)
 
         for b in range(BLOCKS):

@@ -110,7 +110,10 @@ def tile_routed_moe_kernel(tc, xT, w_words, w_scales, gate, offs, out):
             nc.scalar.activation(by_slot(1, piece)[:, :, t], plane_bf16[:, t, :].indirect(offsets_of(piece)), COPY)
 
         def interleave(g, piece):
-            nc.scalar.copy(out=by_slot(g, piece), in_=gathered[g][:, :, piece[0]:piece[1]].rearrange("p t j -> p j t"))
+            nc.scalar.copy(
+                out=by_slot(g, piece).rearrange("p (c i) t -> p c t i", i=4),
+                in_=gathered[g][:, :, piece[0]:piece[1]].rearrange("p t (c i) -> p c t i", i=4),
+            )
 
         def quantize(g, piece):
             nc.vector.quantize_mx(

@@ -43,7 +43,6 @@ def tile_routed_moe_kernel(tc, xT, w_words, w_scales, gate, offs, out):
         psum = ctx.enter_context(tc.psum_pool(name="psum", bufs=1))
 
         offsets = lists.tile([P, SLOTS // PER_COLUMN], U16, name="offsets")
-        nc.sync.dma_start(offsets[:], offs)
 
         scrap_in = keep.tile([P, 8], F32, name="scrap_in")
         scrap_out = keep.tile([P, 8], F32, name="scrap_out")
@@ -56,6 +55,8 @@ def tile_routed_moe_kernel(tc, xT, w_words, w_scales, gate, offs, out):
             columns = WIDE_GATHER_WINDOW if (g, t) in WHOLE_LIST_PLANES else T
             plane[(g, t)] = keep.tile([P, columns], F32, name="plane%d%d" % (g, t))
             nc.sync.dma_start(plane[(g, t)][:, 0:T], x_planes[g, :, t, :])
+            if (g, t) == LOAD_ORDER[0]:
+                nc.sync.dma_start(offsets[:], offs)
 
         w_scale = keep.tile([P, E * PASSES, N], U8, name="w_scale", align_bytes=64)
         nc.vector.memset(w_scale[:].bitcast(I32), 0)
@@ -115,6 +116,10 @@ def tile_routed_moe_kernel(tc, xT, w_words, w_scales, gate, offs, out):
                 in_=gathered[g][:, :, piece[0]:piece[1]].rearrange("p t (c i) -> p c t i", i=4),
             )
 
+        def hold_back(piece, late):
+            for g in range(PASSES):
+                nc.scalar.copy(out=interleaved[g][:, PACK * piece[0]:PACK * (piece[0] + 1)], in_=late[:, 0:PACK])
+
         def quantize(g, piece):
             nc.vector.quantize_mx(
                 out=x_code[g][:, piece[0]:piece[1]].bitcast(FP8X4),
@@ -166,6 +171,7 @@ def tile_routed_moe_kernel(tc, xT, w_words, w_scales, gate, offs, out):
         quantize(1, FIRST)
         multiply(FIRST, 0)
         copy_out(FIRST)
+        hold_back(LAST, sums_sb[(FIRST, BLOCKS - 1)])
 
         gather_f32(0, 3, AFTER_FIRST)
         for t in range(PACK):

@@ -13,6 +13,7 @@ U16 = mybir.dt.uint16
 U8 = mybir.dt.uint8
 FP8X4 = mybir.dt.float8_e4m3fn_x4
 MULT = mybir.AluOpType.mult
+ADD = mybir.AluOpType.add
 COPY = mybir.ActivationFunctionType.Copy
 
 P = 128
@@ -116,9 +117,15 @@ def tile_routed_moe_kernel(tc, xT, w_words, w_scales, gate, offs, out):
                 in_=gathered[g][:, :, piece[0]:piece[1]].rearrange("p t (c i) -> p c t i", i=4),
             )
 
-        def hold_back(piece, late):
-            for g in range(PASSES):
-                nc.scalar.copy(out=interleaved[g][:, PACK * piece[0]:PACK * (piece[0] + 1)], in_=late[:, 0:PACK])
+        def interleave_on_gpsimd(g, piece):
+            nc.gpsimd.tensor_scalar(
+                by_slot(g, piece).rearrange("p (c i) t -> p c t i", i=4),
+                gathered[g][:, :, piece[0]:piece[1]].rearrange("p t (c i) -> p c t i", i=4),
+                1.0,
+                0.0,
+                MULT,
+                ADD,
+            )
 
         def quantize(g, piece):
             nc.vector.quantize_mx(
@@ -171,7 +178,6 @@ def tile_routed_moe_kernel(tc, xT, w_words, w_scales, gate, offs, out):
         quantize(1, FIRST)
         multiply(FIRST, 0)
         copy_out(FIRST)
-        hold_back(LAST, sums_sb[(FIRST, BLOCKS - 1)])
 
         gather_f32(0, 3, AFTER_FIRST)
         for t in range(PACK):
@@ -184,8 +190,8 @@ def tile_routed_moe_kernel(tc, xT, w_words, w_scales, gate, offs, out):
             scatter(FIRST, b)
         copy_out(SECOND)
 
-        interleave(0, LAST)
-        interleave(1, LAST)
+        interleave_on_gpsimd(1, LAST)
+        interleave_on_gpsimd(0, LAST)
         quantize(0, LAST)
         quantize(1, LAST)
         multiply(LAST, 0)

@@ -191,7 +191,8 @@ def tile_routed_moe_kernel(tc, xT, w_words, w_scales, gate, offs, out):
         copy_out(SECOND)
 
         interleave_on_gpsimd(1, LAST)
-        interleave_on_gpsimd(0, LAST)
+        nc.scalar.copy(out=interleaved[0][:, PACK * LAST[0]:PACK * LAST[0] + PACK], in_=sums_sb[(FIRST, BLOCKS - 1)][:, 0:PACK])
+        interleave(0, LAST)
         quantize(0, LAST)
         quantize(1, LAST)
         multiply(LAST, 0)

@@ -32,8 +32,9 @@ WHOLE = (0, 512)
 WIDE_GATHER_WINDOW = 4 * T
 SCATTER_WINDOW = 2 * T
 
-LOAD_ORDER = ((0, 0), (1, 0), (1, 1), (0, 1), (1, 2), (1, 3), (0, 2), (0, 3))
-WHOLE_LIST_PLANES = ((0, 0), (0, 1), (0, 2))
+LOAD_ORDER = ((0, 0), (1, 0), (0, 1), (1, 1), (0, 2), (1, 2), (1, 3), (0, 3))
+WHOLE_LIST_PLANES = ((0, 0), (0, 1), (0, 2), (1, 2), (1, 3))
+HALF = PACK // 2
 
 
 def tile_routed_moe_kernel(tc, xT, w_words, w_scales, gate, offs, out):
@@ -88,7 +89,7 @@ def tile_routed_moe_kernel(tc, xT, w_words, w_scales, gate, offs, out):
             keep.tile([P, PACK, SLOTS], F32, name="gathered0"),
             keep.tile([P, PACK, SLOTS], F32, name="gathered1"),
         ]
-        plane_bf16 = keep.tile([P, PACK, T], BF16, name="plane_bf16")
+        plane_bf16 = keep.tile([P, HALF, T], BF16, name="plane_bf16")
         interleaved = [keep.tile([P, PACK * SLOTS], BF16, name="interleaved%d" % g, align_bytes=64) for g in range(PASSES)]
         x_code = [keep.tile([P, SLOTS], U32, name="x_code%d" % g, align_bytes=64) for g in range(PASSES)]
         x_scale = [keep.tile([P, SLOTS], U8, name="x_scale%d" % g, align_bytes=64) for g in range(PASSES)]
@@ -116,6 +117,20 @@ def tile_routed_moe_kernel(tc, xT, w_words, w_scales, gate, offs, out):
                 out=by_slot(g, piece).rearrange("p (c i) t -> p c t i", i=4),
                 in_=gathered[g][:, :, piece[0]:piece[1]].rearrange("p t (c i) -> p c t i", i=4),
             )
+
+        def upper_pair(piece):
+            return (
+                by_slot(1, piece)[:, :, HALF:PACK].rearrange("p (c i) t -> p c t i", i=4),
+                gathered[1][:, HALF:PACK, piece[0]:piece[1]].rearrange("p t (c i) -> p c t i", i=4),
+            )
+
+        def interleave_pair(piece):
+            pair_out, pair_in = upper_pair(piece)
+            nc.scalar.copy(out=pair_out, in_=pair_in)
+
+        def interleave_pair_on_gpsimd(piece):
+            pair_out, pair_in = upper_pair(piece)
+            nc.gpsimd.tensor_scalar(pair_out, pair_in, 1.0, 0.0, MULT, ADD)
 
         def interleave_on_gpsimd(g, piece):
             nc.gpsimd.tensor_scalar(
@@ -164,37 +179,39 @@ def tile_routed_moe_kernel(tc, xT, w_words, w_scales, gate, offs, out):
                 window[b][:].indirect(offsets_of(piece)), sums_sb[(piece, b)][:], gate_of(piece, b), MULT
             )
 
-
         gather_f32(0, 0, WHOLE)
-        for t in range(PACK):
+        for t in range(HALF):
             round_plane(t)
             gather_bf16(t, FIRST)
             gather_bf16(t, SECOND)
+            gather_bf16(t, LAST)
         gather_f32(0, 1, WHOLE)
         gather_f32(0, 2, WHOLE)
+        gather_f32(1, 2, WHOLE)
+        gather_f32(1, 3, WHOLE)
+        interleave_pair(FIRST)
         gather_f32(0, 3, FIRST)
         interleave(0, FIRST)
-        quantize(0, FIRST)
         quantize(1, FIRST)
+        quantize(0, FIRST)
         multiply(FIRST, 0)
         copy_out(FIRST)
 
         gather_f32(0, 3, AFTER_FIRST)
-        for t in range(PACK):
-            gather_f32(1, t, LAST)
+        interleave_pair(SECOND)
         interleave(0, SECOND)
-        quantize(0, SECOND)
         quantize(1, SECOND)
+        quantize(0, SECOND)
         multiply(SECOND, 1)
         for b in range(BLOCKS):
             scatter(FIRST, b)
         copy_out(SECOND)
 
-        interleave_on_gpsimd(1, LAST)
+        interleave_pair_on_gpsimd(LAST)
         nc.scalar.copy(out=interleaved[0][:, PACK * LAST[0]:PACK * LAST[0] + PACK], in_=sums_sb[(FIRST, BLOCKS - 1)][:, 0:PACK])
         interleave(0, LAST)
-        quantize(0, LAST)
         quantize(1, LAST)
+        quantize(0, LAST)
         multiply(LAST, 0)
         for b in range(BLOCKS):
             scatter(SECOND, b)

@@ -32,9 +32,11 @@ WHOLE = (0, 512)
 WIDE_GATHER_WINDOW = 4 * T
 SCATTER_WINDOW = 2 * T
 
+SCALAR_PLANES = (0, 1)
+VECTOR_PLANES = ((0, PACK), (2, PACK))
+
 LOAD_ORDER = ((0, 0), (1, 0), (0, 1), (1, 1), (0, 2), (1, 2), (1, 3), (0, 3))
 WHOLE_LIST_PLANES = ((0, 0), (0, 1), (0, 2), (1, 2), (1, 3))
-HALF = PACK // 2
 
 
 def tile_routed_moe_kernel(tc, xT, w_words, w_scales, gate, offs, out):
@@ -86,10 +88,9 @@ def tile_routed_moe_kernel(tc, xT, w_words, w_scales, gate, offs, out):
         load_gate(LAST[0], SLOTS)
 
         gathered = [
-            keep.tile([P, PACK, SLOTS], F32, name="gathered0"),
-            keep.tile([P, PACK, SLOTS], F32, name="gathered1"),
+            keep.tile([P, end - first, SLOTS], F32, name="gathered%d" % g) for g, (first, end) in enumerate(VECTOR_PLANES)
         ]
-        plane_bf16 = keep.tile([P, HALF, T], BF16, name="plane_bf16")
+        plane_bf16 = keep.tile([P, len(SCALAR_PLANES), T], BF16, name="plane_bf16")
         interleaved = [keep.tile([P, PACK * SLOTS], BF16, name="interleaved%d" % g, align_bytes=64) for g in range(PASSES)]
         x_code = [keep.tile([P, SLOTS], U32, name="x_code%d" % g, align_bytes=64) for g in range(PASSES)]
         x_scale = [keep.tile([P, SLOTS], U8, name="x_scale%d" % g, align_bytes=64) for g in range(PASSES)]
@@ -104,7 +105,9 @@ def tile_routed_moe_kernel(tc, xT, w_words, w_scales, gate, offs, out):
             return interleaved[g][:, PACK * piece[0]:PACK * piece[1]].rearrange("p (j t) -> p j t", t=PACK)
 
         def gather_f32(g, t, piece):
-            nc.vector.tensor_copy(gathered[g][:, t, piece[0]:piece[1]], plane[(g, t)][:].indirect(offsets_of(piece)))
+            nc.vector.tensor_copy(
+                gathered[g][:, t - VECTOR_PLANES[g][0], piece[0]:piece[1]], plane[(g, t)][:].indirect(offsets_of(piece))
+            )
 
         def round_plane(t):
             nc.scalar.copy(out=plane_bf16[:, t, :], in_=plane[(1, t)][:])
@@ -112,35 +115,20 @@ def tile_routed_moe_kernel(tc, xT, w_words, w_scales, gate, offs, out):
         def gather_bf16(t, piece):
             nc.scalar.activation(by_slot(1, piece)[:, :, t], plane_bf16[:, t, :].indirect(offsets_of(piece)), COPY)
 
-        def interleave(g, piece):
-            nc.scalar.copy(
-                out=by_slot(g, piece).rearrange("p (c i) t -> p c t i", i=4),
-                in_=gathered[g][:, :, piece[0]:piece[1]].rearrange("p t (c i) -> p c t i", i=4),
-            )
-
-        def upper_pair(piece):
+        def interleaving(g, piece):
+            first, end = VECTOR_PLANES[g]
             return (
-                by_slot(1, piece)[:, :, HALF:PACK].rearrange("p (c i) t -> p c t i", i=4),
-                gathered[1][:, HALF:PACK, piece[0]:piece[1]].rearrange("p t (c i) -> p c t i", i=4),
+                by_slot(g, piece)[:, :, first:end].rearrange("p (c i) t -> p c t i", i=4),
+                gathered[g][:, :, piece[0]:piece[1]].rearrange("p t (c i) -> p c t i", i=4),
             )
 
-        def interleave_pair(piece):
-            pair_out, pair_in = upper_pair(piece)
-            nc.scalar.copy(out=pair_out, in_=pair_in)
-
-        def interleave_pair_on_gpsimd(piece):
-            pair_out, pair_in = upper_pair(piece)
-            nc.gpsimd.tensor_scalar(pair_out, pair_in, 1.0, 0.0, MULT, ADD)
+        def interleave(g, piece):
+            destination, source = interleaving(g, piece)
+            nc.scalar.copy(out=destination, in_=source)
 
         def interleave_on_gpsimd(g, piece):
-            nc.gpsimd.tensor_scalar(
-                by_slot(g, piece).rearrange("p (c i) t -> p c t i", i=4),
-                gathered[g][:, :, piece[0]:piece[1]].rearrange("p t (c i) -> p c t i", i=4),
-                1.0,
-                0.0,
-                MULT,
-                ADD,
-            )
+            destination, source = interleaving(g, piece)
+            nc.gpsimd.tensor_scalar(destination, source, 1.0, 0.0, MULT, ADD)
 
         def quantize(g, piece):
             nc.vector.quantize_mx(
@@ -179,8 +167,9 @@ def tile_routed_moe_kernel(tc, xT, w_words, w_scales, gate, offs, out):
                 window[b][:].indirect(offsets_of(piece)), sums_sb[(piece, b)][:], gate_of(piece, b), MULT
             )
 
+
         gather_f32(0, 0, WHOLE)
-        for t in range(HALF):
+        for t in SCALAR_PLANES:
             round_plane(t)
             gather_bf16(t, FIRST)
             gather_bf16(t, SECOND)
@@ -189,7 +178,7 @@ def tile_routed_moe_kernel(tc, xT, w_words, w_scales, gate, offs, out):
         gather_f32(0, 2, WHOLE)
         gather_f32(1, 2, WHOLE)
         gather_f32(1, 3, WHOLE)
-        interleave_pair(FIRST)
+        interleave(1, FIRST)
         gather_f32(0, 3, FIRST)
         interleave(0, FIRST)
         quantize(1, FIRST)
@@ -198,7 +187,7 @@ def tile_routed_moe_kernel(tc, xT, w_words, w_scales, gate, offs, out):
         copy_out(FIRST)
 
         gather_f32(0, 3, AFTER_FIRST)
-        interleave_pair(SECOND)
+        interleave(1, SECOND)
         interleave(0, SECOND)
         quantize(1, SECOND)
         quantize(0, SECOND)
@@ -207,8 +196,8 @@ def tile_routed_moe_kernel(tc, xT, w_words, w_scales, gate, offs, out):
             scatter(FIRST, b)
         copy_out(SECOND)
 
-        interleave_pair_on_gpsimd(LAST)
-        nc.scalar.copy(out=interleaved[0][:, PACK * LAST[0]:PACK * LAST[0] + PACK], in_=sums_sb[(FIRST, BLOCKS - 1)][:, 0:PACK])
+        interleave_on_gpsimd(1, LAST)
+        nc.scalar.copy(out=by_slot(0, LAST)[:, 0, :], in_=sums_sb[(FIRST, BLOCKS - 1)][:, 0:PACK])
         interleave(0, LAST)
         quantize(1, LAST)
         quantize(0, LAST)

from contextlib import ExitStack

import concourse.mybir as mybir

K, T, E, C, N = 1024, 512, 4, 128, 512
FLOPS = 2 * K * N * E * C

F32 = mybir.dt.float32
BF16 = mybir.dt.bfloat16
U32 = mybir.dt.uint32
I32 = mybir.dt.int32
U16 = mybir.dt.uint16
U8 = mybir.dt.uint8
FP8X4 = mybir.dt.float8_e4m3fn_x4
MULT = mybir.AluOpType.mult
ADD = mybir.AluOpType.add
COPY = mybir.ActivationFunctionType.Copy

P = 128
PACK = 4
PASSES = K // (P * PACK)
BLOCKS = N // P
SLOTS = E * C
PER_COLUMN = 16

FIRST = (0, 128)
SECOND = (128, 256)
LAST = (256, 512)
AFTER_FIRST = (128, 512)
WHOLE = (0, 512)

WIDE_GATHER_WINDOW = 4 * T
SCATTER_WINDOW = 2 * T

SCALAR_PLANES = (0, 1)
VECTOR_PLANES = ((0, PACK), (2, PACK))

LOAD_ORDER = ((0, 0), (1, 0), (0, 1), (1, 1), (0, 2), (1, 2), (1, 3), (0, 3))
WHOLE_LIST_PLANES = ((0, 0), (0, 1), (0, 2), (1, 2), (1, 3))


def tile_routed_moe_kernel(tc, xT, w_words, w_scales, gate, offs, out):
    nc = tc.nc
    with ExitStack() as ctx:
        lists = ctx.enter_context(tc.tile_pool(name="lists", bufs=1))
        keep = ctx.enter_context(tc.tile_pool(name="keep", bufs=1))
        psum = ctx.enter_context(tc.psum_pool(name="psum", bufs=1))

        offsets = lists.tile([P, SLOTS // PER_COLUMN], U16, name="offsets")

        scrap_in = keep.tile([P, 8], F32, name="scrap_in")
        scrap_out = keep.tile([P, 8], F32, name="scrap_out")
        nc.gpsimd.memset(scrap_in[:], 0.0)
        nc.scalar.copy(out=scrap_out[:], in_=scrap_in[:])

        x_planes = xT.rearrange("(g p t) n -> g p t n", p=P, t=PACK)
        plane = {}
        for g, t in LOAD_ORDER:
            columns = WIDE_GATHER_WINDOW if (g, t) in WHOLE_LIST_PLANES else T
            plane[(g, t)] = keep.tile([P, columns], F32, name="plane%d%d" % (g, t))
            nc.sync.dma_start(plane[(g, t)][:, 0:T], x_planes[g, :, t, :])
            if (g, t) == LOAD_ORDER[0]:
                nc.sync.dma_start(offsets[:], offs)

        w_scale = keep.tile([P, E * PASSES, N], U8, name="w_scale", align_bytes=64)
        nc.vector.memset(w_scale[:].bitcast(I32), 0)
        scale_rows = w_scales.rearrange("e a (q r) n -> r q (e a) n", r=4)
        for r in range(4):
            nc.sync.dma_start(w_scale[r:P:32, :, :].bitcast(I32), scale_rows[r].bitcast(I32))

        w_code = {}
        gate_sb = {}

        def load_codes(e):
            w_code[e] = keep.tile([P, PASSES, N], U32, name="w_code%d" % e, align_bytes=64)
            nc.sync.dma_start(w_code[e][:].bitcast(I32), w_words[e].rearrange("a p n r -> p a (n r)").bitcast(I32))

        gate_blocks = gate.rearrange("(b p) j -> p b j", p=P)

        def load_gate(first, end):
            gate_sb[first] = keep.tile([P, BLOCKS, end - first], F32, name="gate%d" % first)
            nc.sync.dma_start(gate_sb[first][:], gate_blocks[:, :, first:end])

        load_codes(0)
        load_gate(0, LAST[0])
        for e in range(1, E):
            load_codes(e)
        load_gate(LAST[0], SLOTS)

        gathered = [
            keep.tile([P, end - first, SLOTS], F32, name="gathered%d" % g) for g, (first, end) in enumerate(VECTOR_PLANES)
        ]
        plane_bf16 = keep.tile([P, len(SCALAR_PLANES), T], BF16, name="plane_bf16")
        interleaved = [keep.tile([P, PACK * SLOTS], BF16, name="interleaved%d" % g, align_bytes=64) for g in range(PASSES)]
        x_code = [keep.tile([P, SLOTS], U32, name="x_code%d" % g, align_bytes=64) for g in range(PASSES)]
        x_scale = [keep.tile([P, SLOTS], U8, name="x_scale%d" % g, align_bytes=64) for g in range(PASSES)]
        window = [keep.tile([P, SCATTER_WINDOW], F32, name="window%d" % b) for b in range(BLOCKS)]
        sums = {}
        sums_sb = {}

        def offsets_of(piece):
            return offsets[:, piece[0] // PER_COLUMN:piece[1] // PER_COLUMN]

        def by_slot(g, piece):
            return interleaved[g][:, PACK * piece[0]:PACK * piece[1]].rearrange("p (j t) -> p j t", t=PACK)

        def gather_f32(g, t, piece):
            nc.vector.tensor_copy(
                gathered[g][:, t - VECTOR_PLANES[g][0], piece[0]:piece[1]], plane[(g, t)][:].indirect(offsets_of(piece))
            )

        def round_plane(t):
            nc.scalar.copy(out=plane_bf16[:, t, :], in_=plane[(1, t)][:])

        def gather_bf16(t, piece):
            nc.scalar.activation(by_slot(1, piece)[:, :, t], plane_bf16[:, t, :].indirect(offsets_of(piece)), COPY)

        def interleaving(g, piece):
            first, end = VECTOR_PLANES[g]
            return (
                by_slot(g, piece)[:, :, first:end].rearrange("p (c i) t -> p c t i", i=4),
                gathered[g][:, :, piece[0]:piece[1]].rearrange("p t (c i) -> p c t i", i=4),
            )

        def interleave(g, piece):
            destination, source = interleaving(g, piece)
            nc.scalar.copy(out=destination, in_=source)

        def interleave_on_gpsimd(g, piece):
            destination, source = interleaving(g, piece)
            nc.gpsimd.tensor_scalar(destination, source, 1.0, 0.0, MULT, ADD)

        def quantize(g, piece):
            nc.vector.quantize_mx(
                out=x_code[g][:, piece[0]:piece[1]].bitcast(FP8X4),
                scales=x_scale[g][:, piece[0]:piece[1]],
                in_=interleaved[g][:, PACK * piece[0]:PACK * piece[1]],
            )

        def multiply(piece, banks):
            for b in range(BLOCKS):
                sums[(piece, b)] = psum.tile([P, 512], F32, name="sums_%d_%d" % (banks, b))
                for e in range(piece[0] // C, piece[1] // C):
                    slots = slice(e * C, (e + 1) * C)
                    for g in range(PASSES):
                        nc.tensor.matmul_mx(
                            out=sums[(piece, b)][:, e * C - piece[0]:(e + 1) * C - piece[0]],
                            lhsT=w_code[e][:, g, b * P:(b + 1) * P].bitcast(FP8X4),
                            lhsT_scale=w_scale[:, e * PASSES + g, b * P:(b + 1) * P],
                            rhs=x_code[g][:, slots].bitcast(FP8X4),
                            rhs_scale=x_scale[g][:, slots],
                            start=(g == 0),
                            stop=(g == PASSES - 1),
                        )

        def copy_out(piece):
            for b in range(BLOCKS):
                sums_sb[(piece, b)] = keep.tile([P, piece[1] - piece[0]], F32, name="sums_sb_%d_%d" % (piece[0], b))
                nc.scalar.copy(out=sums_sb[(piece, b)][:], in_=sums[(piece, b)][:, 0:piece[1] - piece[0]])

        def gate_of(piece, b):
            first = 0 if piece[0] < LAST[0] else LAST[0]
            return gate_sb[first][:, b, piece[0] - first:piece[1] - first]

        def scatter(piece, b):
            nc.vector.tensor_tensor(
                window[b][:].indirect(offsets_of(piece)), sums_sb[(piece, b)][:], gate_of(piece, b), MULT
            )


        gather_f32(0, 0, WHOLE)
        for t in SCALAR_PLANES:
            round_plane(t)
            gather_bf16(t, FIRST)
            gather_bf16(t, SECOND)
            gather_bf16(t, LAST)
        gather_f32(0, 1, WHOLE)
        gather_f32(0, 2, WHOLE)
        gather_f32(1, 2, WHOLE)
        gather_f32(1, 3, WHOLE)
        interleave(1, FIRST)
        gather_f32(0, 3, FIRST)
        interleave(0, FIRST)
        quantize(1, FIRST)
        quantize(0, FIRST)
        multiply(FIRST, 0)
        copy_out(FIRST)

        gather_f32(0, 3, AFTER_FIRST)
        interleave(1, SECOND)
        interleave(0, SECOND)
        quantize(1, SECOND)
        quantize(0, SECOND)
        multiply(SECOND, 1)
        for b in range(BLOCKS):
            scatter(FIRST, b)
        copy_out(SECOND)

        interleave_on_gpsimd(1, LAST)
        nc.scalar.copy(out=by_slot(0, LAST)[:, 0, :], in_=sums_sb[(FIRST, BLOCKS - 1)][:, 0:PACK])
        interleave(0, LAST)
        quantize(1, LAST)
        quantize(0, LAST)
        multiply(LAST, 0)
        for b in range(BLOCKS):
            scatter(SECOND, b)
        copy_out(LAST)

        for b in range(BLOCKS):
            scatter(LAST, b)
            nc.sync.dma_start(out[b * P:(b + 1) * P, :], window[b][:, 0:T])
